import numpy as np
CORES = [1,3,5,9,11,13]
N = 6
R, T, B = 16384, 4096, 128
def entries(a): return a.T.reshape(-1)
def pack(v, P): return np.ascontiguousarray(np.asarray(v, np.int32).reshape(-1, P).T)
def lists(rng, how):
    I = rng.integers(0, N * R, (N, T)); E = np.sort(rng.integers(0, T + 1, (N, B)), axis=1)
    if how == "void":
        E = np.zeros((N, B), np.int64)
        for r in range(N): k = np.sort(1 + rng.permutation(B - 2)[:6]); c = np.sort(1 + rng.permutation(T)[:6]); E[r] = np.concatenate([[0], c])[np.searchsorted(k, np.arange(B), side="right")]
        E[rng.integers(N)] = 0
    if how == "one":
        p = rng.permutation(N); z = rng.integers(0, B, N); z[p[0]] = 0; z[p[1]] = B - 1; E = np.where(np.arange(B)[None, :] < z[:, None], 0, T)
        I[p[::2]] = R * p[1] + I[p[::2]] % R
    if how == "single": E = np.broadcast_to(1 + np.arange(B), (N, B)).copy()
    if how == "hotrank": I = R * int(rng.integers(N)) + rng.integers(0, R, (N, T))
    if how == "edge":
        for r in range(N): I[r, rng.permutation(T)[:8 * N]] = np.tile(np.concatenate([R * np.arange(N), R * np.arange(N) + R - 1]), 4)
        E[:, -1] = T
    return {"idx": np.stack([pack(i, 16) for i in I]), "end": np.stack([pack(v, 16) for v in E])}
def setup_inputs(rng):
    return dict({"tab": rng.standard_normal((N, 128, R), dtype=np.float32)}, **lists(rng, "uniform"))
def setup_inputs_edge(rng):
    d = setup_inputs(rng); d.update(lists(rng, "edge"))
    for k in ("tab",): d[k] = (d[k].astype(np.float32) * 1024.0).astype(d[k].dtype)
    return d
def setup_inputs_hotrank(rng):
    d = setup_inputs(rng); d.update(lists(rng, "hotrank"))
    for k in ("tab",): d[k] = (d[k].astype(np.float32) * (1 / 1024.0)).astype(d[k].dtype)
    return d
def setup_inputs_one(rng):
    d = setup_inputs(rng); d.update(lists(rng, "one"))
    return d
def setup_inputs_single(rng):
    d = setup_inputs(rng); d.update(lists(rng, "single"))
    return d
def setup_inputs_void(rng):
    d = setup_inputs(rng); d.update(lists(rng, "void"))
    return d
def check_inputs(x):
    bad = []
    if x["idx"].min() < 0 or x["idx"].max() >= N * R: bad.append("idx out of range")
    if x["end"].min() < 0 or x["end"].max() >= T + 1: bad.append("end out of range")
    if any((np.diff(entries(a)) < 0).any() for a in x["end"]): bad.append("end falls")
    return bad
def reference(tab, idx, end):
    A = np.concatenate(list(tab), axis=1).astype(np.float64)
    y = np.zeros((N, 128, B), np.float64)
    for r in range(N):
        G = A[:, entries(idx[r])]; c = np.concatenate([[0], entries(end[r])])
        for b in range(B):
            if c[b + 1] > c[b]: y[r][:, b] = G[:, c[b]:c[b + 1]].sum(axis=1)
    return {"y": y.astype(np.float32)}

@@ -1,0 +1,306 @@
+from concourse.bass import DstId, RemoteDMATransfer
+from concourse.mybir import AluOpType, ActivationFunctionType
+
+R, NL, ENT, NB = 16384, 6, 4096, 128
+CORES_SIM = 16
+ST = 1376
+HALF = ST // 2
+OC = ST // 16
+SC = OC + 2
+LC = 3 * SC
+EC = 10
+LK = 144
+PW = LC + 2 * EC
+PWP = PW + 4
+WIN = (3, R + 5)
+
+SCRATCH = {
+    "win": ("sbuf", [128, R + 8], "float32"),
+    "ones": ("sbuf", [128, 384], "float32"),
+    "sel": ("sbuf", [128, 10 * 128], "float32"),
+    "idxi": ("sbuf", [128, 256], "int32"),
+    "idxf": ("sbuf", [128, LC], "float32"),
+    "endi": ("sbuf", [128, 12], "int32"),
+    "endf": ("sbuf", [128, 12], "float32"),
+    "psl": ("psum", [128, 512], "float32"),
+    "pse": ("psum", [128, 512], "float32"),
+    "ki": ("sbuf", [128, EC], "int32"),
+    "kap": ("sbuf", [128, EC], "uint16"),
+    "snd": ("sbuf", [128, PW], "float32"),
+    "lrx": ("sbuf", [128, PW], "float32"),
+    "add1": ("sbuf", [128, LK], "float32"),
+    "add2": ("sbuf", [128, LK], "float32"),
+    "add3": ("sbuf", [128, LK], "float32"),
+    "tt": ("sbuf", [128, NB + 4], "float32"),
+    "yv": ("sbuf", [128, NB], "float32"),
+}
+FAMILIES = {
+    "e": (6, 12, "float32"), "pt": (5, LC, "float32"), "pay": (5, PWP, "uint16"), "lp": (3, LK, "float32"),
+    "rl": (3, LK, "float32"), "ofs": (NL, PWP, "uint16"), "pf": (NL, 4 + ST, "float32"), "sa": (NL, 4 + 2 * ST, "float32"),
+    "st": (NL, ST, "float32"), "rm": (NL, LK, "float32"), "qq": (NL, LK, "float32"),
+}
+for _f in FAMILIES:
+    SCRATCH[_f] = ("sbuf", [128, FAMILIES[_f][0] * FAMILIES[_f][1]], FAMILIES[_f][2])
+
+SEMAPHORES = ["d_idx", "d_end", "tab", "ones", "iot", "sel", "idxf", "endf", "pe_e", "pe_l", "vc", "sndl", "snde", "sent",
+              "ms", "relu", "own", "loc", "larr", "pyoff", "pyon", "rarr", "lp0", "lp1", "lp2", "fin", "yst"]
+SEMAPHORES += ["pk%d" % k for k in range(5)] + ["lo%d" % k for k in range(NL)]
+SEMAPHORES += ["%s_%d" % (p, k) for p in ("S0", "S2", "T2", "A", "P", "R", "Q") for k in range(NL)]
+
+SX = [1152, 0, 1376, 1376, 1376, 1056]
+SCALAR = "S0_0 S0_1 S0_2 R_0 S2_2 S2_0 R_1 R_2 S0_3 S0_4 S2_3 S0_5 S2_4 R_3 R_4 S2_5 R_5".split()
+VECTOR = ("T2_0 T2_1 A_0 A_1 A_2 P0_1 P1_1 P0_2 P1_2 P0_0 P1_0 Q_1 Q_2 A_3 Q_0 A_4 P0_3 P1_3 A_5 P0_4 P1_4 Q_3 Q_4 "
+          "T2_5 ADD1 P0_5 ADD2 P1_5 ADD3 Q_5").split()
+SENDS = [1, 2, 0, 3, 4]
+
+
+def piece(T, f, k, a=0, b=None):
+    w = FAMILIES[f][1]
+    return T[f][:, k * w + a:k * w + (w if b is None else b)]
+
+
+def layout(core, T, topo):
+    here = [r for r, c in enumerate(T.cores) if topo.chip(c) == topo.chip(core)]
+    away = [r for r, c in enumerate(T.cores) if topo.chip(c) != topo.chip(core)]
+    relays = [c for c in range(CORES_SIM) if topo.chip(c) == topo.chip(core) and T.rank_of(c) is None
+              and all(topo.may_write(c, T.cores[r]) for r in away)]
+    return here, away, relays[:len(here)]
+
+
+def bits(mask):
+    return [1 << b for b in range(mask.bit_length()) if mask >> b & 1]
+
+
+def dst(topo, c):
+    rid, pid, _ = topo.addr(c)
+    return DstId(rid=rid, pnc=pid)
+
+
+def offsets(g, T, src, rank, tmp, f, k, relu, done):
+    g.scalar.activation(out=tmp, in_=src[:, 0:LC], func=ActivationFunctionType.Relu,
+                        bias=float(1 - R * rank)).then_inc(relu, 1)
+    g.vector.wait_ge(relu, 1)
+    g.vector.tensor_scalar(out=piece(T, f, k, 0, LC), in0=tmp, scalar1=float(R + 1), scalar2=None,
+                           op0=AluOpType.min).then_inc(done, 1)
+    g.vector.tensor_copy(out=piece(T, f, k, LC, PW), in_=src[:, LC:PW]).then_inc(done, 1)
+
+
+def relay_program(g, core, T, topo, here, away, me):
+    sem = T.sem
+    mine = here[me]
+    low = bits(topo.mask(core, T.cores[away[0]]))
+    dests = away + [r for r in here if r != mine]
+    g.scalar.wait_ge(sem.larr, len(low))
+    g.vector.wait_ge(sem.larr, len(low))
+    for k, r in enumerate(dests):
+        offsets(g, T, T.lrx, r, piece(T, "pt", k), "pay", k, sem["pk%d" % k],
+                sem.pyoff if r in away else sem.pyon)
+    loc = 0
+    for group, ready in ((away, sem.pyoff), (dests[len(away):], sem.pyon)):
+        n = 2 if len(group) > 2 else 4
+        g.wait_ge(ready, 2 * len(group))
+        tr = []
+        for j, r in enumerate(group):
+            m = sum(low[j * n:(j + 1) * n])
+            tr.append(RemoteDMATransfer(dst_ids=[dst(topo, T.cores[r])], dma_engine_mask=m, remote_sem=sem["lo%d" % mine],
+                                        src=piece(T, "pay", dests.index(r), 0, PW), dst=piece(T, "ofs", mine, 0, PW)))
+            loc += n
+        g.remote_dma_fused(tr, local_sem=sem.loc)
+    g.wait_ge(sem.rarr, len(low) * len(here))
+    g.remote_dma_fused([RemoteDMATransfer(dst_ids=[dst(topo, T.cores[away[me]])], dma_engine_mask=sum(low),
+                                          remote_sem=sem.lp2, srcs=[piece(T, "rl", k) for k in range(len(here))],
+                                          dsts=[piece(T, "lp", 2)], alu_op=1)], local_sem=sem.loc)
+    g.wait_ge(sem.loc, loc + len(low))
+
+
+def rank_program(g, core, T, topo):
+    here, away, relays = layout(core, T, topo)
+    rank = T.rank_of(core)
+    if rank is None:
+        if core in relays:
+            relay_program(g, core, T, topo, here, away, relays.index(core))
+        return
+    sem = T.sem
+    me = here.index(rank)
+    low = bits(topo.mask(core, T.cores[away[0]]))
+    E, NE = sum(low), len(low)
+
+    g.sync.dma_start(T.idxi[0:16, :], T.idx[:]).then_inc(sem.d_idx, 16)
+    g.scalar.dma_start(T.endi[0:16, 0:8], T.end[:]).then_inc(sem.d_end, 16)
+    for k in range(8):
+        if k == 3:
+            g.sync.wait_ge(sem.sent, 1)
+        g.sync.dma_start(T.win[k::8, 4:R + 4], T.tab[k::8, :]).then_inc(sem.tab, 16)
+
+    g.vector.memset(T.ones[0:16, :], 1.0).then_inc(sem.ones, 1)
+    g.vector.memset(T.idxf[0:16, 256:LC], -1.0).then_inc(sem.idxf, 1)
+    zeros = [T.win[:, 0:4], T.win[:, R + 4:R + 8], T.tt[:, 0:4]]
+    for n in range(NL):
+        zeros += [piece(T, "pf", n, 0, 4), piece(T, "sa", n, 0, 4)]
+
+    g.iota(T.endi[0:16, 8:12], [[0, 4]], 0, 3 * HALF).then_inc(sem.iot, 1)
+    g.wait_ge(sem.ones, 1)
+    g.affine_select(T.sel[0:16, 9 * 128:], T.ones[0:16, 0:128], [[0, 8], [-1, 16]], AluOpType.is_equal, 0.0, 0,
+                    1).then_inc(sem.sel, 1)
+    for s in range(3):
+        g.affine_select(T.sel[0:16, s * 384:(s + 1) * 384], T.ones[0:16, :], [[16, 3], [0, 8], [-3, 16]],
+                        AluOpType.is_equal, 0.0, -s, 1).then_inc(sem.sel, 1)
+
+    v = g.vector
+    v.wait_ge(sem.d_end, 16)
+    v.wait_ge(sem.iot, 1)
+    v.tensor_scalar(out=T.endf[0:16, :], in0=T.endi[0:16, :], scalar1=float(3 * ST), scalar2=None,
+                    op0=AluOpType.min).then_inc(sem.endf, 1)
+    v.wait_ge(sem.d_idx, 16)
+    v.tensor_copy(out=T.idxf[0:16, 0:256], in_=T.idxi[0:16, :]).then_inc(sem.idxf, 1)
+
+    te = g.tensor
+    te.wait_ge(sem.sel, 4)
+    te.wait_ge(sem.endf, 1)
+    te.matmul(T.pse[:, 0:EC], T.sel[0:16, 9 * 128:], T.endf[0:16, 0:EC], True, True).then_inc(sem.pe_e, 1)
+    te.wait_ge(sem.idxf, 2)
+    for s in range(3):
+        for q in range(3):
+            mm = te.matmul(T.psl[:, s * SC:(s + 1) * SC], T.sel[0:16, (3 * s + q) * 128:(3 * s + q + 1) * 128],
+                           T.idxf[0:16, q:LC:3], q == 0, q == 2)
+    mm.then_inc(sem.pe_l, 1)
+
+    cnt = [0]
+
+    def chain(call):
+        call.then_inc(sem.vc, 1)
+        cnt[0] += 1
+        v.wait_ge(sem.vc, cnt[0])
+
+    def es(k):
+        return piece(T, "e", k, 0, EC)
+
+    pe, kf = T.pse[:, 0:EC], T.snd[:, LC:LC + EC]
+    v.wait_ge(sem.pe_e, 1)
+    chain(v.tensor_scalar(out=es(0), in0=pe, scalar1=1.0, scalar2=1.0 / 3.0, op0=AluOpType.subtract, op1=AluOpType.mult))
+    chain(v.tensor_copy(out=T.ki[:], in_=es(0)))
+    chain(v.tensor_copy(out=kf, in_=T.ki[:]))
+    chain(v.tensor_scalar(out=es(1), in0=kf, scalar1=-3.0, scalar2=None, op0=AluOpType.mult))
+    chain(v.tensor_tensor(out=es(2), in0=es(1), in1=pe, op=AluOpType.add))
+    v.tensor_scalar(out=es(5), in0=es(2), scalar1=0.0, scalar2=None, op0=AluOpType.is_gt).then_inc(sem.vc, 1)
+    cnt[0] += 1
+    chain(v.tensor_scalar(out=es(3), in0=es(2), scalar1=float(ST), scalar2=float(1 - ST), op0=AluOpType.mult,
+                          op1=AluOpType.add))
+    chain(v.tensor_tensor(out=es(4), in0=es(3), in1=kf, op=AluOpType.add))
+    v.tensor_tensor(out=T.snd[:, LC + EC:PW], in0=es(4), in1=es(5), op=AluOpType.mult).then_inc(sem.snde, 1)
+    v.wait_ge(sem.pe_l, 1)
+    v.tensor_copy(out=T.snd[:, 0:LC], in_=T.psl[:, 0:LC]).then_inc(sem.sndl, 1)
+
+    g.wait_ge(sem.snde, 1)
+    g.wait_ge(sem.sndl, 1)
+    rid, pid, _ = topo.addr(relays[me])
+    g.remote_dma(T.lrx[:], T.snd[:], sem.larr, sem.loc, pid, rid, E)
+    g.sem_inc(sem.sent, 1)
+    loc = NE
+
+    for z in zeros:
+        v.memset(z, 0.0).then_inc(sem.ms, 1)
+    g.scalar.wait_ge(sem.sndl, 1)
+    g.scalar.wait_ge(sem.snde, 1)
+    v.wait_ge(sem.sndl, 1)
+    v.wait_ge(sem.snde, 1)
+    offsets(g, T, T.snd, rank, piece(T, "pt", 0), "ofs", rank, sem.relu, sem.own)
+    v.tensor_scalar(out=T.kap[:], in0=kf, scalar1=HALF + 0.5, scalar2=None, op0=AluOpType.is_gt).then_inc(sem.own, 1)
+
+    order = away + [here[(me + d) % len(here)] for d in range(1, len(here))] + [rank]
+    win = T.win[:, WIN[0]:WIN[1]]
+    seen = {"s": set(), "v": set()}
+
+    def need(eng, key, name, val):
+        if name not in seen[key]:
+            seen[key].add(name)
+            eng.wait_ge(sem[name], val)
+
+    def start(eng, key, n):
+        need(eng, key, "tab", 128)
+        need(eng, key, "ms", len(zeros))
+        r = order[n]
+        if r == rank:
+            need(eng, key, "own", 3)
+        else:
+            need(eng, key, "lo%d" % r, 2 if r in away else 4)
+
+    def off(n, a, b):
+        return piece(T, "ofs", order[n], a, b)
+
+    for op in SCALAR:
+        p, n = op.split("_")
+        n = int(n)
+        start(g.scalar, "s", n)
+        if p == "S0":
+            out, src = piece(T, "sa", n, 4, 4 + ST), win.indirect(off(n, 0, OC))
+        elif p == "S2":
+            out, src = piece(T, "st", n, 0, SX[n]), win.indirect(off(n, 2 * SC, 2 * SC + SX[n] // 16))
+        else:
+            need(g.scalar, "s", "S0_%d" % n, 1)
+            need(g.scalar, "s", "A_%d" % n, 1)
+            out, src = piece(T, "rm", n), piece(T, "sa", n, 3, 4 + 2 * ST).indirect(off(n, LC + EC, LC + EC + LK // 16))
+        g.scalar.activation(out=out, in_=src, func=ActivationFunctionType.Copy).then_inc(sem[op], 1)
+
+    for op in VECTOR:
+        if op == "ADD1":
+            v.wait_ge(sem.lp2, NE)
+            v.wait_ge(sem.lp0, NE)
+            chain(v.tensor_tensor(out=T.add1[:], in0=piece(T, "lp", 2), in1=piece(T, "lp", 0), op=AluOpType.add))
+            continue
+        if op == "ADD2":
+            need(v, "v", "R_5", 1)
+            chain(v.tensor_tensor(out=T.add2[:], in0=T.add1[:], in1=piece(T, "rm", NL - 1), op=AluOpType.add))
+            continue
+        if op == "ADD3":
+            v.wait_ge(sem.lp1, NE)
+            chain(v.tensor_tensor(out=T.add3[:], in0=T.add2[:], in1=piece(T, "lp", 1), op=AluOpType.add))
+            continue
+        p, n = op.split("_")
+        n = int(n)
+        start(v, "v", n)
+        if p == "T2":
+            v.tensor_copy(out=piece(T, "st", n, SX[n], ST),
+                          in_=win.indirect(off(n, 2 * SC + SX[n] // 16, 2 * SC + OC))).then_inc(sem[op], 1)
+        elif p == "A":
+            need(v, "v", "S0_%d" % n, 1)
+            v.tensor_tensor(out=piece(T, "sa", n, 4 + ST, 4 + 2 * ST), in0=win.indirect(off(n, SC, SC + OC)),
+                            in1=piece(T, "sa", n, 4, 4 + ST), op=AluOpType.add).then_inc(sem[op], 1)
+        elif p in ("P0", "P1"):
+            a = HALF * int(p[1])
+            need(v, "v", "A_%d" % n, 1)
+            if SX[n] > a:
+                need(v, "v", "S2_%d" % n, 1)
+            if SX[n] < a + HALF:
+                need(v, "v", "T2_%d" % n, 1)
+            v.tensor_tensor_scan(piece(T, "pf", n, 4 + a, 4 + a + HALF), piece(T, "sa", n, 4 + ST + a, 4 + ST + a + HALF),
+                                 piece(T, "st", n, a, a + HALF), 0.0,
+                                 AluOpType.add, AluOpType.add).then_inc(sem["P_%d" % n], 1)
+        else:
+            v.wait_ge(sem["P_%d" % n], 2)
+            need(v, "v", "R_%d" % n, 1)
+            rest = T.add3[:] if n == NL - 1 else piece(T, "rm", n)
+            v.tensor_tensor(out=piece(T, "qq", n), in0=piece(T, "pf", n, 3, 4 + ST).indirect(off(n, LC, LC + LK // 16)),
+                            in1=rest, op=AluOpType.add).then_inc(sem[op], 1)
+
+    for n in SENDS:
+        r = order[n]
+        if r in away:
+            to, land, arr = relays[away.index(r)], piece(T, "rl", me), sem.rarr
+        else:
+            k = n - len(away)
+            to, land, arr = T.cores[r], piece(T, "lp", k), sem["lp%d" % k]
+        g.wait_ge(sem["Q_%d" % n], 1)
+        rid, pid, _ = topo.addr(to)
+        g.remote_dma(land, piece(T, "qq", n), arr, sem.loc, pid, rid, E)
+        loc += NE
+
+    last = NL - 1
+    v.wait_ge(sem["Q_%d" % last], 1)
+    chain(v.tensor_tensor(out=T.tt[:, 4:4 + NB], in0=piece(T, "qq", last, NB, NB + 2).indirect(T.kap[:, 0:NB // 16]),
+                          in1=piece(T, "qq", last, 0, NB), op=AluOpType.add))
+    v.tensor_tensor(out=T.yv[:], in0=T.tt[:, 4:4 + NB], in1=T.tt[:, 3:3 + NB], op=AluOpType.subtract).then_inc(sem.fin, 1)
+    g.sync.wait_ge(sem.fin, 1)
+    g.sync.dma_start(T.y[:], T.yv[:]).then_inc(sem.yst, 16)
+    g.sync.wait_ge(sem.yst, 16)
+    g.wait_ge(sem.loc, loc)

@@ -13,6 +13,7 @@ LK = 144
 PW = LC + 2 * EC
 PWP = PW + 4
 WIN = (3, R + 5)
+PIECES, AHEAD, PACED = 16, 5, 10
 
 SCRATCH = {
     "win": ("sbuf", [128, R + 8], "float32"),
@@ -42,16 +43,17 @@ FAMILIES = {
 for _f in FAMILIES:
     SCRATCH[_f] = ("sbuf", [128, FAMILIES[_f][0] * FAMILIES[_f][1]], FAMILIES[_f][2])
 
-SEMAPHORES = ["d_idx", "d_end", "tab", "ones", "iot", "sel", "idxf", "endf", "pe_e", "pe_l", "vc", "sndl", "snde", "sent",
+SEMAPHORES = ["d_idx", "d_end", "tab", "ones", "iot", "selr", "idxf", "endf", "pe_e", "pe_l", "vc", "sndl", "snde", "sent",
               "ms", "relu", "own", "loc", "larr", "pyoff", "pyon", "rarr", "lp0", "lp1", "lp2", "fin", "yst"]
-SEMAPHORES += ["pk%d" % k for k in range(5)] + ["lo%d" % k for k in range(NL)]
+SEMAPHORES += ["pk%d" % k for k in range(5)] + ["lo%d" % k for k in range(NL)] + ["sel%d" % k for k in range(3)]
+SEMAPHORES += ["t%d" % k for k in range(AHEAD)]
 SEMAPHORES += ["%s_%d" % (p, k) for p in ("S0", "S2", "T2", "A", "P", "R", "Q") for k in range(NL)]
 
-SX = [1152, 0, 1376, 1376, 1376, 1056]
-SCALAR = "S0_0 S0_1 S0_2 R_0 S2_2 S2_0 R_1 R_2 S0_3 S0_4 S2_3 S0_5 S2_4 R_3 R_4 S2_5 R_5".split()
-VECTOR = ("T2_0 T2_1 A_0 A_1 A_2 P0_1 P1_1 P0_2 P1_2 P0_0 P1_0 Q_1 Q_2 A_3 Q_0 A_4 P0_3 P1_3 A_5 P0_4 P1_4 Q_3 Q_4 "
-          "T2_5 ADD1 P0_5 ADD2 P1_5 ADD3 Q_5").split()
-SENDS = [1, 2, 0, 3, 4]
+SX = [1024, 0, 1376, 1376, 1376, 832]
+SCALAR = "S0_5 S0_0 S0_1 S0_2 S2_2 S2_0 R_2 S0_3 S0_4 R_0 R_1 S2_3 S2_4 R_4 R_3 S2_5 R_5".split()
+VECTOR = ("T2_5 T2_1 T2_0 A_0 A_1 A_2 P0_1 P1_1 P0_2 P1_2 P0_0 P1_0 Q_2 A_3 Q_0 Q_1 A_4 P0_3 P1_3 P0_4 P1_4 Q_3 Q_4 "
+          "A_5 ADD1 P0_5 ADD2 P1_5 ADD3 Q_5").split()
+SENDS = [2, 0, 1, 3, 4]
 
 
 def piece(T, f, k, a=0, b=None):
@@ -76,13 +78,10 @@ def dst(topo, c):
     return DstId(rid=rid, pnc=pid)
 
 
-def offsets(g, T, src, rank, tmp, f, k, relu, done):
-    g.scalar.activation(out=tmp, in_=src[:, 0:LC], func=ActivationFunctionType.Relu,
-                        bias=float(1 - R * rank)).then_inc(relu, 1)
+def offsets(g, src, rank, tmp, out, relu, done):
+    g.scalar.activation(out=tmp, in_=src, func=ActivationFunctionType.Relu, bias=float(1 - R * rank)).then_inc(relu, 1)
     g.vector.wait_ge(relu, 1)
-    g.vector.tensor_scalar(out=piece(T, f, k, 0, LC), in0=tmp, scalar1=float(R + 1), scalar2=None,
-                           op0=AluOpType.min).then_inc(done, 1)
-    g.vector.tensor_copy(out=piece(T, f, k, LC, PW), in_=src[:, LC:PW]).then_inc(done, 1)
+    g.vector.tensor_scalar(out=out, in0=tmp, scalar1=float(R + 1), scalar2=None, op0=AluOpType.min).then_inc(done, 1)
 
 
 def relay_program(g, core, T, topo, here, away, me):
@@ -90,15 +89,17 @@ def relay_program(g, core, T, topo, here, away, me):
     mine = here[me]
     low = bits(topo.mask(core, T.cores[away[0]]))
     dests = away + [r for r in here if r != mine]
+    ready = [sem.pyoff if r in away else sem.pyon for r in dests]
     g.scalar.wait_ge(sem.larr, len(low))
     g.vector.wait_ge(sem.larr, len(low))
+    for k in range(len(dests)):
+        g.vector.tensor_copy(out=piece(T, "pay", k, LC, PW), in_=T.lrx[:, LC:PW]).then_inc(ready[k], 1)
     for k, r in enumerate(dests):
-        offsets(g, T, T.lrx, r, piece(T, "pt", k), "pay", k, sem["pk%d" % k],
-                sem.pyoff if r in away else sem.pyon)
+        offsets(g, T.lrx[:, 0:LC], r, piece(T, "pt", k), piece(T, "pay", k, 0, LC), sem["pk%d" % k], ready[k])
     loc = 0
-    for group, ready in ((away, sem.pyoff), (dests[len(away):], sem.pyon)):
+    for group, done in ((away, sem.pyoff), (dests[len(away):], sem.pyon)):
         n = 2 if len(group) > 2 else 4
-        g.wait_ge(ready, 2 * len(group))
+        g.wait_ge(done, 2 * len(group))
         tr = []
         for j, r in enumerate(group):
             m = sum(low[j * n:(j + 1) * n])
@@ -127,10 +128,12 @@ def rank_program(g, core, T, topo):
 
     g.sync.dma_start(T.idxi[0:16, :], T.idx[:]).then_inc(sem.d_idx, 16)
     g.scalar.dma_start(T.endi[0:16, 0:8], T.end[:]).then_inc(sem.d_end, 16)
-    for k in range(8):
-        if k == 3:
+    for k in range(PIECES):
+        if AHEAD <= k < PACED:
+            g.sync.wait_ge(sem["t%d" % (k - AHEAD)], 16)
+        if k == PACED:
             g.sync.wait_ge(sem.sent, 1)
-        g.sync.dma_start(T.win[k::8, 4:R + 4], T.tab[k::8, :]).then_inc(sem.tab, 16)
+        g.sync.dma_start(T.win[k::PIECES, 4:R + 4], T.tab[k::PIECES, :]).then_inc(sem["t%d" % k] if k < AHEAD else sem.tab, 16)
 
     g.vector.memset(T.ones[0:16, :], 1.0).then_inc(sem.ones, 1)
     g.vector.memset(T.idxf[0:16, 256:LC], -1.0).then_inc(sem.idxf, 1)
@@ -138,13 +141,17 @@ def rank_program(g, core, T, topo):
     for n in range(NL):
         zeros += [piece(T, "pf", n, 0, 4), piece(T, "sa", n, 0, 4)]
 
+    def select(s):
+        g.affine_select(T.sel[0:16, s * 384:(s + 1) * 384], T.ones[0:16, :], [[16, 3], [0, 8], [-3, 16]],
+                        AluOpType.is_equal, 0.0, -s, 1).then_inc(sem["sel%d" % s], 1)
+
     g.iota(T.endi[0:16, 8:12], [[0, 4]], 0, 3 * HALF).then_inc(sem.iot, 1)
     g.wait_ge(sem.ones, 1)
+    select(0)
     g.affine_select(T.sel[0:16, 9 * 128:], T.ones[0:16, 0:128], [[0, 8], [-1, 16]], AluOpType.is_equal, 0.0, 0,
-                    1).then_inc(sem.sel, 1)
-    for s in range(3):
-        g.affine_select(T.sel[0:16, s * 384:(s + 1) * 384], T.ones[0:16, :], [[16, 3], [0, 8], [-3, 16]],
-                        AluOpType.is_equal, 0.0, -s, 1).then_inc(sem.sel, 1)
+                    1).then_inc(sem.selr, 1)
+    select(1)
+    select(2)
 
     v = g.vector
     v.wait_ge(sem.d_end, 16)
@@ -155,11 +162,12 @@ def rank_program(g, core, T, topo):
     v.tensor_copy(out=T.idxf[0:16, 0:256], in_=T.idxi[0:16, :]).then_inc(sem.idxf, 1)
 
     te = g.tensor
-    te.wait_ge(sem.sel, 4)
+    te.wait_ge(sem.selr, 1)
     te.wait_ge(sem.endf, 1)
     te.matmul(T.pse[:, 0:EC], T.sel[0:16, 9 * 128:], T.endf[0:16, 0:EC], True, True).then_inc(sem.pe_e, 1)
     te.wait_ge(sem.idxf, 2)
     for s in range(3):
+        te.wait_ge(sem["sel%d" % s], 1)
         for q in range(3):
             mm = te.matmul(T.psl[:, s * SC:(s + 1) * SC], T.sel[0:16, (3 * s + q) * 128:(3 * s + q + 1) * 128],
                            T.idxf[0:16, q:LC:3], q == 0, q == 2)
@@ -198,14 +206,14 @@ def rank_program(g, core, T, topo):
     g.sem_inc(sem.sent, 1)
     loc = NE
 
-    for z in zeros:
-        v.memset(z, 0.0).then_inc(sem.ms, 1)
     g.scalar.wait_ge(sem.sndl, 1)
-    g.scalar.wait_ge(sem.snde, 1)
     v.wait_ge(sem.sndl, 1)
     v.wait_ge(sem.snde, 1)
-    offsets(g, T, T.snd, rank, piece(T, "pt", 0), "ofs", rank, sem.relu, sem.own)
+    v.tensor_copy(out=piece(T, "ofs", rank, LC, PW), in_=T.snd[:, LC:PW]).then_inc(sem.own, 1)
     v.tensor_scalar(out=T.kap[:], in0=kf, scalar1=HALF + 0.5, scalar2=None, op0=AluOpType.is_gt).then_inc(sem.own, 1)
+    offsets(g, T.snd[:, 0:LC], rank, piece(T, "pt", 0), piece(T, "ofs", rank, 0, LC), sem.relu, sem.own)
+    for z in zeros:
+        v.memset(z, 0.0).then_inc(sem.ms, 1)
 
     order = away + [here[(me + d) % len(here)] for d in range(1, len(here))] + [rank]
     win = T.win[:, WIN[0]:WIN[1]]
@@ -217,8 +225,8 @@ def rank_program(g, core, T, topo):
             eng.wait_ge(sem[name], val)
 
     def start(eng, key, n):
-        need(eng, key, "tab", 128)
         need(eng, key, "ms", len(zeros))
+        need(eng, key, "tab", 16 * (PIECES - AHEAD))
         r = order[n]
         if r == rank:
             need(eng, key, "own", 3)

from concourse.bass import DstId, RemoteDMATransfer
from concourse.mybir import AluOpType, ActivationFunctionType

R, NL, ENT, NB = 16384, 6, 4096, 128
CORES_SIM = 16
ST = 1376
HALF = ST // 2
OC = ST // 16
SC = OC + 2
LC = 3 * SC
EC = 10
LK = 144
PW = LC + 2 * EC
PWP = PW + 4
WIN = (3, R + 5)
PIECES, AHEAD, PACED = 16, 5, 10

SCRATCH = {
    "win": ("sbuf", [128, R + 8], "float32"),
    "ones": ("sbuf", [128, 384], "float32"),
    "sel": ("sbuf", [128, 10 * 128], "float32"),
    "idxi": ("sbuf", [128, 256], "int32"),
    "idxf": ("sbuf", [128, LC], "float32"),
    "endi": ("sbuf", [128, 12], "int32"),
    "endf": ("sbuf", [128, 12], "float32"),
    "psl": ("psum", [128, 512], "float32"),
    "pse": ("psum", [128, 512], "float32"),
    "ki": ("sbuf", [128, EC], "int32"),
    "kap": ("sbuf", [128, EC], "uint16"),
    "snd": ("sbuf", [128, PW], "float32"),
    "lrx": ("sbuf", [128, PW], "float32"),
    "add1": ("sbuf", [128, LK], "float32"),
    "add2": ("sbuf", [128, LK], "float32"),
    "add3": ("sbuf", [128, LK], "float32"),
    "tt": ("sbuf", [128, NB + 4], "float32"),
    "yv": ("sbuf", [128, NB], "float32"),
}
FAMILIES = {
    "e": (6, 12, "float32"), "pt": (5, LC, "float32"), "pay": (5, PWP, "uint16"), "lp": (3, LK, "float32"),
    "rl": (3, LK, "float32"), "ofs": (NL, PWP, "uint16"), "pf": (NL, 4 + ST, "float32"), "sa": (NL, 4 + 2 * ST, "float32"),
    "st": (NL, ST, "float32"), "rm": (NL, LK, "float32"), "qq": (NL, LK, "float32"),
}
for _f in FAMILIES:
    SCRATCH[_f] = ("sbuf", [128, FAMILIES[_f][0] * FAMILIES[_f][1]], FAMILIES[_f][2])

SEMAPHORES = ["d_idx", "d_end", "tab", "ones", "iot", "selr", "idxf", "endf", "pe_e", "pe_l", "vc", "sndl", "snde", "sent",
              "ms", "relu", "own", "loc", "larr", "pyoff", "pyon", "rarr", "lp0", "lp1", "lp2", "fin", "yst"]
SEMAPHORES += ["pk%d" % k for k in range(5)] + ["lo%d" % k for k in range(NL)] + ["sel%d" % k for k in range(3)]
SEMAPHORES += ["t%d" % k for k in range(AHEAD)]
SEMAPHORES += ["%s_%d" % (p, k) for p in ("S0", "S2", "T2", "A", "P", "R", "Q") for k in range(NL)]

SX = [1024, 0, 1376, 1376, 1376, 832]
SCALAR = "S0_5 S0_0 S0_1 S0_2 S2_2 S2_0 R_2 S0_3 S0_4 R_0 R_1 S2_3 S2_4 R_4 R_3 S2_5 R_5".split()
VECTOR = ("T2_5 T2_1 T2_0 A_0 A_1 A_2 P0_1 P1_1 P0_2 P1_2 P0_0 P1_0 Q_2 A_3 Q_0 Q_1 A_4 P0_3 P1_3 P0_4 P1_4 Q_3 Q_4 "
          "A_5 ADD1 P0_5 ADD2 P1_5 ADD3 Q_5").split()
SENDS = [2, 0, 1, 3, 4]


def piece(T, f, k, a=0, b=None):
    w = FAMILIES[f][1]
    return T[f][:, k * w + a:k * w + (w if b is None else b)]


def layout(core, T, topo):
    here = [r for r, c in enumerate(T.cores) if topo.chip(c) == topo.chip(core)]
    away = [r for r, c in enumerate(T.cores) if topo.chip(c) != topo.chip(core)]
    relays = [c for c in range(CORES_SIM) if topo.chip(c) == topo.chip(core) and T.rank_of(c) is None
              and all(topo.may_write(c, T.cores[r]) for r in away)]
    return here, away, relays[:len(here)]


def bits(mask):
    return [1 << b for b in range(mask.bit_length()) if mask >> b & 1]


def dst(topo, c):
    rid, pid, _ = topo.addr(c)
    return DstId(rid=rid, pnc=pid)


def offsets(g, src, rank, tmp, out, relu, done):
    g.scalar.activation(out=tmp, in_=src, func=ActivationFunctionType.Relu, bias=float(1 - R * rank)).then_inc(relu, 1)
    g.vector.wait_ge(relu, 1)
    g.vector.tensor_scalar(out=out, in0=tmp, scalar1=float(R + 1), scalar2=None, op0=AluOpType.min).then_inc(done, 1)


def relay_program(g, core, T, topo, here, away, me):
    sem = T.sem
    mine = here[me]
    low = bits(topo.mask(core, T.cores[away[0]]))
    dests = away + [r for r in here if r != mine]
    ready = [sem.pyoff if r in away else sem.pyon for r in dests]
    g.scalar.wait_ge(sem.larr, len(low))
    g.vector.wait_ge(sem.larr, len(low))
    for k in range(len(dests)):
        g.vector.tensor_copy(out=piece(T, "pay", k, LC, PW), in_=T.lrx[:, LC:PW]).then_inc(ready[k], 1)
    for k, r in enumerate(dests):
        offsets(g, T.lrx[:, 0:LC], r, piece(T, "pt", k), piece(T, "pay", k, 0, LC), sem["pk%d" % k], ready[k])
    loc = 0
    for group, done in ((away, sem.pyoff), (dests[len(away):], sem.pyon)):
        n = 2 if len(group) > 2 else 4
        g.wait_ge(done, 2 * len(group))
        tr = []
        for j, r in enumerate(group):
            m = sum(low[j * n:(j + 1) * n])
            tr.append(RemoteDMATransfer(dst_ids=[dst(topo, T.cores[r])], dma_engine_mask=m, remote_sem=sem["lo%d" % mine],
                                        src=piece(T, "pay", dests.index(r), 0, PW), dst=piece(T, "ofs", mine, 0, PW)))
            loc += n
        g.remote_dma_fused(tr, local_sem=sem.loc)
    g.wait_ge(sem.rarr, len(low) * len(here))
    g.remote_dma_fused([RemoteDMATransfer(dst_ids=[dst(topo, T.cores[away[me]])], dma_engine_mask=sum(low),
                                          remote_sem=sem.lp2, srcs=[piece(T, "rl", k) for k in range(len(here))],
                                          dsts=[piece(T, "lp", 2)], alu_op=1)], local_sem=sem.loc)
    g.wait_ge(sem.loc, loc + len(low))


def rank_program(g, core, T, topo):
    here, away, relays = layout(core, T, topo)
    rank = T.rank_of(core)
    if rank is None:
        if core in relays:
            relay_program(g, core, T, topo, here, away, relays.index(core))
        return
    sem = T.sem
    me = here.index(rank)
    low = bits(topo.mask(core, T.cores[away[0]]))
    E, NE = sum(low), len(low)

    g.sync.dma_start(T.idxi[0:16, :], T.idx[:]).then_inc(sem.d_idx, 16)
    g.scalar.dma_start(T.endi[0:16, 0:8], T.end[:]).then_inc(sem.d_end, 16)
    for k in range(PIECES):
        if AHEAD <= k < PACED:
            g.sync.wait_ge(sem["t%d" % (k - AHEAD)], 16)
        if k == PACED:
            g.sync.wait_ge(sem.sent, 1)
        g.sync.dma_start(T.win[k::PIECES, 4:R + 4], T.tab[k::PIECES, :]).then_inc(sem["t%d" % k] if k < AHEAD else sem.tab, 16)

    g.vector.memset(T.ones[0:16, :], 1.0).then_inc(sem.ones, 1)
    g.vector.memset(T.idxf[0:16, 256:LC], -1.0).then_inc(sem.idxf, 1)
    zeros = [T.win[:, 0:4], T.win[:, R + 4:R + 8], T.tt[:, 0:4]]
    for n in range(NL):
        zeros += [piece(T, "pf", n, 0, 4), piece(T, "sa", n, 0, 4)]

    def select(s):
        g.affine_select(T.sel[0:16, s * 384:(s + 1) * 384], T.ones[0:16, :], [[16, 3], [0, 8], [-3, 16]],
                        AluOpType.is_equal, 0.0, -s, 1).then_inc(sem["sel%d" % s], 1)

    g.iota(T.endi[0:16, 8:12], [[0, 4]], 0, 3 * HALF).then_inc(sem.iot, 1)
    g.wait_ge(sem.ones, 1)
    select(0)
    g.affine_select(T.sel[0:16, 9 * 128:], T.ones[0:16, 0:128], [[0, 8], [-1, 16]], AluOpType.is_equal, 0.0, 0,
                    1).then_inc(sem.selr, 1)
    select(1)
    select(2)

    v = g.vector
    v.wait_ge(sem.d_end, 16)
    v.wait_ge(sem.iot, 1)
    v.tensor_scalar(out=T.endf[0:16, :], in0=T.endi[0:16, :], scalar1=float(3 * ST), scalar2=None,
                    op0=AluOpType.min).then_inc(sem.endf, 1)
    v.wait_ge(sem.d_idx, 16)
    v.tensor_copy(out=T.idxf[0:16, 0:256], in_=T.idxi[0:16, :]).then_inc(sem.idxf, 1)

    te = g.tensor
    te.wait_ge(sem.selr, 1)
    te.wait_ge(sem.endf, 1)
    te.matmul(T.pse[:, 0:EC], T.sel[0:16, 9 * 128:], T.endf[0:16, 0:EC], True, True).then_inc(sem.pe_e, 1)
    te.wait_ge(sem.idxf, 2)
    for s in range(3):
        te.wait_ge(sem["sel%d" % s], 1)
        for q in range(3):
            mm = te.matmul(T.psl[:, s * SC:(s + 1) * SC], T.sel[0:16, (3 * s + q) * 128:(3 * s + q + 1) * 128],
                           T.idxf[0:16, q:LC:3], q == 0, q == 2)
    mm.then_inc(sem.pe_l, 1)

    cnt = [0]

    def chain(call):
        call.then_inc(sem.vc, 1)
        cnt[0] += 1
        v.wait_ge(sem.vc, cnt[0])

    def es(k):
        return piece(T, "e", k, 0, EC)

    pe, kf = T.pse[:, 0:EC], T.snd[:, LC:LC + EC]
    v.wait_ge(sem.pe_e, 1)
    chain(v.tensor_scalar(out=es(0), in0=pe, scalar1=1.0, scalar2=1.0 / 3.0, op0=AluOpType.subtract, op1=AluOpType.mult))
    chain(v.tensor_copy(out=T.ki[:], in_=es(0)))
    chain(v.tensor_copy(out=kf, in_=T.ki[:]))
    chain(v.tensor_scalar(out=es(1), in0=kf, scalar1=-3.0, scalar2=None, op0=AluOpType.mult))
    chain(v.tensor_tensor(out=es(2), in0=es(1), in1=pe, op=AluOpType.add))
    v.tensor_scalar(out=es(5), in0=es(2), scalar1=0.0, scalar2=None, op0=AluOpType.is_gt).then_inc(sem.vc, 1)
    cnt[0] += 1
    chain(v.tensor_scalar(out=es(3), in0=es(2), scalar1=float(ST), scalar2=float(1 - ST), op0=AluOpType.mult,
                          op1=AluOpType.add))
    chain(v.tensor_tensor(out=es(4), in0=es(3), in1=kf, op=AluOpType.add))
    v.tensor_tensor(out=T.snd[:, LC + EC:PW], in0=es(4), in1=es(5), op=AluOpType.mult).then_inc(sem.snde, 1)
    v.wait_ge(sem.pe_l, 1)
    v.tensor_copy(out=T.snd[:, 0:LC], in_=T.psl[:, 0:LC]).then_inc(sem.sndl, 1)

    g.wait_ge(sem.snde, 1)
    g.wait_ge(sem.sndl, 1)
    rid, pid, _ = topo.addr(relays[me])
    g.remote_dma(T.lrx[:], T.snd[:], sem.larr, sem.loc, pid, rid, E)
    g.sem_inc(sem.sent, 1)
    loc = NE

    g.scalar.wait_ge(sem.sndl, 1)
    v.wait_ge(sem.sndl, 1)
    v.wait_ge(sem.snde, 1)
    v.tensor_copy(out=piece(T, "ofs", rank, LC, PW), in_=T.snd[:, LC:PW]).then_inc(sem.own, 1)
    v.tensor_scalar(out=T.kap[:], in0=kf, scalar1=HALF + 0.5, scalar2=None, op0=AluOpType.is_gt).then_inc(sem.own, 1)
    offsets(g, T.snd[:, 0:LC], rank, piece(T, "pt", 0), piece(T, "ofs", rank, 0, LC), sem.relu, sem.own)
    for z in zeros:
        v.memset(z, 0.0).then_inc(sem.ms, 1)

    order = away + [here[(me + d) % len(here)] for d in range(1, len(here))] + [rank]
    win = T.win[:, WIN[0]:WIN[1]]
    seen = {"s": set(), "v": set()}

    def need(eng, key, name, val):
        if name not in seen[key]:
            seen[key].add(name)
            eng.wait_ge(sem[name], val)

    def start(eng, key, n):
        need(eng, key, "ms", len(zeros))
        need(eng, key, "tab", 16 * (PIECES - AHEAD))
        r = order[n]
        if r == rank:
            need(eng, key, "own", 3)
        else:
            need(eng, key, "lo%d" % r, 2 if r in away else 4)

    def off(n, a, b):
        return piece(T, "ofs", order[n], a, b)

    for op in SCALAR:
        p, n = op.split("_")
        n = int(n)
        start(g.scalar, "s", n)
        if p == "S0":
            out, src = piece(T, "sa", n, 4, 4 + ST), win.indirect(off(n, 0, OC))
        elif p == "S2":
            out, src = piece(T, "st", n, 0, SX[n]), win.indirect(off(n, 2 * SC, 2 * SC + SX[n] // 16))
        else:
            need(g.scalar, "s", "S0_%d" % n, 1)
            need(g.scalar, "s", "A_%d" % n, 1)
            out, src = piece(T, "rm", n), piece(T, "sa", n, 3, 4 + 2 * ST).indirect(off(n, LC + EC, LC + EC + LK // 16))
        g.scalar.activation(out=out, in_=src, func=ActivationFunctionType.Copy).then_inc(sem[op], 1)

    for op in VECTOR:
        if op == "ADD1":
            v.wait_ge(sem.lp2, NE)
            v.wait_ge(sem.lp0, NE)
            chain(v.tensor_tensor(out=T.add1[:], in0=piece(T, "lp", 2), in1=piece(T, "lp", 0), op=AluOpType.add))
            continue
        if op == "ADD2":
            need(v, "v", "R_5", 1)
            chain(v.tensor_tensor(out=T.add2[:], in0=T.add1[:], in1=piece(T, "rm", NL - 1), op=AluOpType.add))
            continue
        if op == "ADD3":
            v.wait_ge(sem.lp1, NE)
            chain(v.tensor_tensor(out=T.add3[:], in0=T.add2[:], in1=piece(T, "lp", 1), op=AluOpType.add))
            continue
        p, n = op.split("_")
        n = int(n)
        start(v, "v", n)
        if p == "T2":
            v.tensor_copy(out=piece(T, "st", n, SX[n], ST),
                          in_=win.indirect(off(n, 2 * SC + SX[n] // 16, 2 * SC + OC))).then_inc(sem[op], 1)
        elif p == "A":
            need(v, "v", "S0_%d" % n, 1)
            v.tensor_tensor(out=piece(T, "sa", n, 4 + ST, 4 + 2 * ST), in0=win.indirect(off(n, SC, SC + OC)),
                            in1=piece(T, "sa", n, 4, 4 + ST), op=AluOpType.add).then_inc(sem[op], 1)
        elif p in ("P0", "P1"):
            a = HALF * int(p[1])
            need(v, "v", "A_%d" % n, 1)
            if SX[n] > a:
                need(v, "v", "S2_%d" % n, 1)
            if SX[n] < a + HALF:
                need(v, "v", "T2_%d" % n, 1)
            v.tensor_tensor_scan(piece(T, "pf", n, 4 + a, 4 + a + HALF), piece(T, "sa", n, 4 + ST + a, 4 + ST + a + HALF),
                                 piece(T, "st", n, a, a + HALF), 0.0,
                                 AluOpType.add, AluOpType.add).then_inc(sem["P_%d" % n], 1)
        else:
            v.wait_ge(sem["P_%d" % n], 2)
            need(v, "v", "R_%d" % n, 1)
            rest = T.add3[:] if n == NL - 1 else piece(T, "rm", n)
            v.tensor_tensor(out=piece(T, "qq", n), in0=piece(T, "pf", n, 3, 4 + ST).indirect(off(n, LC, LC + LK // 16)),
                            in1=rest, op=AluOpType.add).then_inc(sem[op], 1)

    for n in SENDS:
        r = order[n]
        if r in away:
            to, land, arr = relays[away.index(r)], piece(T, "rl", me), sem.rarr
        else:
            k = n - len(away)
            to, land, arr = T.cores[r], piece(T, "lp", k), sem["lp%d" % k]
        g.wait_ge(sem["Q_%d" % n], 1)
        rid, pid, _ = topo.addr(to)
        g.remote_dma(land, piece(T, "qq", n), arr, sem.loc, pid, rid, E)
        loc += NE

    last = NL - 1
    v.wait_ge(sem["Q_%d" % last], 1)
    chain(v.tensor_tensor(out=T.tt[:, 4:4 + NB], in0=piece(T, "qq", last, NB, NB + 2).indirect(T.kap[:, 0:NB // 16]),
                          in1=piece(T, "qq", last, 0, NB), op=AluOpType.add))
    v.tensor_tensor(out=T.yv[:], in0=T.tt[:, 4:4 + NB], in1=T.tt[:, 3:3 + NB], op=AluOpType.subtract).then_inc(sem.fin, 1)
    g.sync.wait_ge(sem.fin, 1)
    g.sync.dma_start(T.y[:], T.yv[:]).then_inc(sem.yst, 16)
    g.sync.wait_ge(sem.yst, 16)
    g.wait_ge(sem.loc, loc)
